import numpy as np
import ml_dtypes


def mxq(x, axis, fmt="e4m3"):
    dtype, down = {"e4m3": (ml_dtypes.float8_e4m3fn, 7), "e5m2": (ml_dtypes.float8_e5m2, 14)}[fmt]
    v = np.moveaxis(np.asarray(x, np.float32).astype(ml_dtypes.bfloat16).astype(np.float64), axis, -1)
    blocks = v.reshape(v.shape[:-1] + (-1, 32))
    amax = np.abs(blocks).max(-1, keepdims=True)
    byte = np.maximum(np.where(amax > 0, np.frexp(amax)[1] - 1 + 127, 0) - down, 1)
    scale = np.exp2(byte - 127.0)
    codes = (blocks / scale).astype(np.float32).astype(dtype).astype(np.float64)
    return np.moveaxis((codes * scale).reshape(v.shape), -1, axis)


WIDE = False


def mx_kscale(k):
    if not WIDE:
        return np.ones(k)
    levels = np.array([10, -10, 5, -5, 0])
    if k % 512:
        return np.exp2(np.random.permutation(np.resize(levels, k // 32))).repeat(32)
    a = np.empty((k // 512, 16))
    for p in range(k // 512):
        a[p, :8] = np.random.permutation(np.resize(levels, 8))
        for g in range(8):
            far = levels[np.abs(levels - a[p, g]) >= 10]
            a[p, g + 8] = far[np.random.randint(len(far))]
    return np.exp2(a.ravel()).repeat(32)


def f64(x):
    return np.asarray(x).astype(np.float64)


def striped(idx):
    return np.tile(np.asarray(idx).reshape(-1, 16).T, (8, 1)).astype(np.uint16)


def unstriped(offs):
    return offs[:16].T.reshape(-1).astype(np.int64)


E2M1 = np.array([0.0, 0.5, 1.0, 1.5, 2.0, 3.0, 4.0, 6.0, -0.0, -0.5, -1.0, -1.5, -2.0, -3.0, -4.0, -6.0])


def pack_weight(w, fmt):
    k, n = w.shape
    w = f64(np.asarray(w, np.float32).astype(ml_dtypes.bfloat16)).reshape(k // 32, 32, n)
    amax = np.abs(w).max(1)
    if fmt == "e4m3":
        byte = np.frexp(amax)[1] - 1 + 127 - 7
    else:
        mant, ex = np.frexp(amax / 6.0)
        byte = np.where(mant > 0.5, ex, ex - 1) + 127
    byte = np.clip(np.where(amax > 0, byte, 1), 1, 254)
    scaled = (w * np.exp2(127.0 - byte)[:, None, :]).reshape(k, n).astype(np.float32)
    by_word = np.ascontiguousarray(scaled.reshape(k // 512, 128, 4, n).transpose(0, 1, 3, 2))
    if fmt == "e4m3":
        words = by_word.astype(ml_dtypes.float8_e4m3fn).view(np.uint8)
    else:
        c = by_word.astype(ml_dtypes.float4_e2m1fn).view(np.uint8) & 0xF
        words = (c[..., 0::2] | (c[..., 1::2] << 4)).reshape(k // 512, 128, 2 * n)
    return np.ascontiguousarray(words), np.ascontiguousarray(byte.astype(np.uint8).reshape(k // 512, 16, n))


def unpack_weight(words, scales, fmt):
    g, _, n = scales.shape
    words = np.ascontiguousarray(words).reshape(g, 128, n, -1)
    if fmt == "e4m3":
        vals = words.view(ml_dtypes.float8_e4m3fn).astype(np.float64)
    else:
        nib = np.empty((g, 128, n, 4), np.uint8)
        nib[..., 0::2] = words & 0xF
        nib[..., 1::2] = words >> 4
        vals = E2M1[nib]
    vals = vals * np.repeat(np.exp2(scales.astype(np.float64) - 127.0), 8, axis=1)[..., None]
    return vals.transpose(0, 1, 3, 2).reshape(g * 512, n)


D, K, R, T, I, Q, G = 512, 512, 512, 2048, 512, 128, 64


def setup_inputs():
    n = np.random.standard_normal
    idx = np.random.permutation(T)[:I]
    fd = mx_kscale(D)
    fk = mx_kscale(K)
    fr = mx_kscale(R)
    keysp = pack_weight(n((D, T)) / fd[:, None], "e4m3")
    tabp = pack_weight(n((K, T)) / fk[:, None], "e4m3")
    return {
        "query": (n((D, Q)) * 0.6 / np.sqrt(D) * fd[:, None]).astype(np.float32),
        "keys_words": keysp[0],
        "keys_scales": keysp[1],
        "sharp": (np.random.uniform(1.0, 3.0, (Q, 1))).astype(np.float32),
        "tab_words": tabp[0],
        "tab_scales": tabp[1],
        "w1": (n((K, R)) * 1 / np.sqrt(K) * fk[:, None]).astype(np.float32),
        "gain": (np.random.uniform(0.5, 2.0, (R, 1))).astype(np.float32),
        "gout": (n((R, Q)) * 1 / np.sqrt(R) * fr[:, None]).astype(np.float32),
        "hsc": (np.random.uniform(0.7, 1.4, (R, 1)) / fr[:, None]).astype(np.float32),
        "old": (0.5 * n((Q, T))).astype(np.float32),
        "offs": striped(idx),
    }


def reference(query, keys_words, keys_scales, sharp, tab_words, tab_scales, w1, gain, gout, hsc, old, offs):
    idx = unstriped(offs)
    keysu = unpack_weight(keys_words, keys_scales, "e4m3")
    tabu = unpack_weight(tab_words, tab_scales, "e4m3")
    queryq = mxq(f64(query), 0, "e4m3")
    keysidxg = keysu[:, idx]
    a = queryq.T @ keysidxg
    p = np.exp(a)
    s = p.reshape(Q, G, I // G).sum(axis=2)
    ms = a.reshape(Q, G, I // G).mean(axis=2) * f64(sharp)
    pg = np.exp(ms - np.max(ms, axis=1, keepdims=True))
    z = np.sum(pg, axis=1, keepdims=True)
    sh = pg / z / s
    rr = np.repeat(sh, I // G, axis=1)
    w1q = mxq(f64(w1), 0, "e4m3")
    tabidxg = tabu[:, idx]
    zh = w1q.T @ tabidxg
    ht = np.tanh(zh)
    hv = ht * f64(gain)
    hs1 = hv * f64(hsc)
    goutq = mxq(f64(gout), 0, "e4m3")
    hs1q = mxq(hs1, 0, "e4m3")
    c0 = goutq.T @ hs1q
    drr = c0 * p
    dsh = drr.reshape(Q, G, I // G).sum(axis=2)
    dz = np.sum(dsh / s * pg / np.square(z) * (-1.0), axis=1, keepdims=True)
    dpg = dsh / s / z + dz
    dms = dpg * pg
    e1 = dms * f64(sharp) / 8.0
    r1 = np.repeat(e1, I // G, axis=1)
    ds = dsh * pg / z / np.square(s) * (-1.0)
    r2 = np.repeat(ds, I // G, axis=1)
    dp = c0 * rr + r2
    da = r1 + dp * p
    gs = da * 512.0
    gf = np.zeros((Q, T))
    gf[:, idx] = gs
    y = f64(old) + gf
    return y

@@ -1,0 +1,184 @@
+from contextlib import ExitStack
+
+import concourse.mybir as mybir
+
+D, K, R, T, I, Q, G = 512, 512, 512, 2048, 512, 128, 64
+FLOPS = 2 * D * Q * I + 2 * K * R * I + 2 * R * Q * I
+
+F32 = mybir.dt.float32
+BF16 = mybir.dt.bfloat16
+I32 = mybir.dt.int32
+U32 = mybir.dt.uint32
+U16 = mybir.dt.uint16
+U8 = mybir.dt.uint8
+FP8X4 = mybir.dt.float8_e4m3fn_x4
+ALU = mybir.AluOpType
+ACT = mybir.ActivationFunctionType
+AX = mybir.AxisListType
+
+P = 128
+PACK = 4
+GS = I // G
+CHUNK = 128
+HALF = I // 2
+TAB_ROW = 4
+OUT_PIECE = 512
+
+
+def tile_attend_blrgained_bygroup_kernel(tc, query, keys_words, keys_scales, sharp, tab_words, tab_scales, w1, gain, gout, hsc, old, offs, out):
+    nc = tc.nc
+
+    with ExitStack() as ctx:
+        sb = ctx.enter_context(tc.tile_pool(name="sb", bufs=1))
+        ps = ctx.enter_context(tc.psum_pool(name="ps", bufs=1))
+
+        def rep(ap, groups):
+            return ap.unsqueeze(2).to_broadcast([P, groups, GS])
+
+        def grouped(ap):
+            return ap.rearrange("p (g e) -> p g e", e=GS)
+
+        def load_scales(queue, plane, scales, first):
+            for r in range(4):
+                queue.dma_start(plane[first + r : P : 32, :].bitcast(I32), scales[0, r:16:4, :].bitcast(I32))
+
+        def quantise(name, inter, width):
+            codes = sb.tile([P, width], U32, name=name + "_codes", align_bytes=64)
+            scales = sb.tile([P, width], U8, name=name + "_scales", align_bytes=64)
+            nc.vector.quantize_mx(out=codes[:].bitcast(FP8X4), scales=scales[:], in_=inter)
+            return codes, scales
+
+        offsets = sb.tile([P, I // 16], U16, name="offsets")
+        nc.sync.dma_start(offsets[:], offs)
+
+        kscale = sb.tile([P, T], U8, name="kscale", align_bytes=64)
+        tscale = sb.tile([P, T], U8, name="tscale", align_bytes=64)
+        nc.vector.memset(kscale[:].bitcast(I32), 0)
+        nc.vector.memset(tscale[:].bitcast(I32), 0)
+        window = sb.tile([P, T], F32, name="window")
+        nc.vector.memset(window[:], 0.0)
+        load_scales(nc.scalar, kscale, keys_scales, 0)
+
+        qraw = sb.tile([P, PACK, Q], F32, name="qraw", tag="raw")
+        nc.sync.dma_start(qraw[:], query.rearrange("(p j) q -> p j q", j=PACK))
+        kwords = sb.tile([P, T], I32, name="kwords", tag="keys", align_bytes=64)
+        nc.sync.dma_start(kwords[:], keys_words[0].rearrange("p n t -> p (n t)").bitcast(I32))
+        wraw = []
+        for h in range(2):
+            wr = sb.tile([P, PACK, R // 2], F32, name=f"wraw{h}")
+            nc.sync.dma_start(wr[:], w1[:, h * R // 2 : (h + 1) * R // 2].rearrange("(p j) r -> p j r", j=PACK))
+            wraw.append(wr)
+        twords = sb.tile([P, T], I32, name="twords", tag="tab")
+        nc.sync.dma_start(twords[:], tab_words[0].rearrange("p n t -> p (n t)").bitcast(I32))
+
+        sharp_sb = sb.tile([P, 1], F32, name="sharp_sb")
+        nc.gpsimd.dma_start(sharp_sb[:], sharp)
+        load_scales(nc.gpsimd, tscale, tab_scales, TAB_ROW)
+        gain_sb = sb.tile([P, PACK], F32, name="gain_sb")
+        nc.gpsimd.dma_start(gain_sb[:], gain.rearrange("(p j) o -> p (j o)", j=PACK))
+        hsc_sb = sb.tile([P, PACK], F32, name="hsc_sb")
+        nc.gpsimd.dma_start(hsc_sb[:], hsc.rearrange("(p j) o -> p (j o)", j=PACK))
+        gh = sb.tile([P, PACK], F32, name="gh")
+        nc.gpsimd.tensor_tensor(gh[:], gain_sb[:], hsc_sb[:], ALU.mult)
+
+        sh8 = sb.tile([P, 1], F32, name="sh8")
+        nc.scalar.activation(sh8[:], sharp_sb[:], ACT.Identity, scale=1.0 / GS)
+        nsh8 = sb.tile([P, 1], F32, name="nsh8")
+        nc.scalar.activation(nsh8[:], sharp_sb[:], ACT.Identity, scale=-1.0 / GS)
+
+        ksg = sb.tile([P, I], U8, name="ksg", align_bytes=64)
+        nc.vector.tensor_copy(ksg[:], kscale[:].indirect(offsets[:]))
+        kwg = sb.tile([P, I], U32, name="kwg", align_bytes=64)
+        nc.vector.tensor_copy(kwg[:], kwords[:].bitcast(U32).indirect(offsets[:]))
+        qint = sb.tile([P, Q * PACK], BF16, name="qint", align_bytes=64)
+        nc.scalar.copy(qint[:].rearrange("p (c i j) -> p c j i", i=4, j=PACK), qraw[:].rearrange("p j (c i) -> p c j i", i=4))
+        qc, qs = quantise("q", qint[:], Q)
+        a_ps = ps.tile([P, I], F32, name="a_ps")
+        nc.tensor.matmul_mx(out=a_ps[:], lhsT=qc[:].bitcast(FP8X4), lhsT_scale=qs[:], rhs=kwg[:].bitcast(FP8X4), rhs_scale=ksg[:], start=True, stop=True)
+        p_sb = sb.tile([P, I], F32, name="p_sb")
+        nc.scalar.activation(p_sb[:], a_ps[:], ACT.Exp)
+
+        graw = sb.tile([P, PACK, Q], F32, name="graw", tag="raw")
+        nc.sync.dma_start(graw[:], gout.rearrange("(p j) q -> p j q", j=PACK))
+
+        tsg = sb.tile([P, I], U8, name="tsg", tag="keys", align_bytes=64)
+        nc.vector.tensor_copy(tsg[:], tscale[:].indirect(offsets[:]))
+        wint = sb.tile([P, R * PACK], BF16, name="wint", align_bytes=64)
+        wv_out = wint[:].rearrange("p (t m j) -> p m t j", t=PACK, j=PACK)
+        for h in range(2):
+            nc.scalar.copy(wv_out[:, 64 * h : 64 * (h + 1)], wraw[h][:].rearrange("p j (m t) -> p m t j", t=PACK))
+        wc, ws = quantise("w", wint[:], R)
+        twg = []
+        for h in range(2):
+            tw = sb.tile([P, HALF], U32, name=f"twg{h}", align_bytes=64)
+            nc.vector.tensor_copy(tw[:], twords[:].bitcast(U32).indirect(offsets[:, 16 * h : 16 * (h + 1)]))
+            twg.append(tw)
+
+        gint = sb.tile([P, Q * PACK], BF16, name="gint", align_bytes=64)
+        nc.scalar.copy(gint[:].rearrange("p (c i j) -> p c j i", i=4, j=PACK), graw[:].rearrange("p j (c i) -> p c j i", i=4))
+        gc, gsc = quantise("g", gint[:], Q)
+
+        c_ps = [ps.tile([P, HALF], F32, name=f"c_ps{h}") for h in range(2)]
+        for c in range(I // CHUNK):
+            h, e = divmod(c, 2)
+            cols = slice(e * CHUNK, (e + 1) * CHUNK)
+            zh = ps.tile([P, PACK, CHUNK], F32, name=f"zh{c}")
+            for t in range(PACK):
+                m = slice(t * P, (t + 1) * P)
+                nc.tensor.matmul_mx(out=zh[:, t, :], lhsT=wc[:, m].bitcast(FP8X4), lhsT_scale=ws[:, m], rhs=twg[h][:, cols].bitcast(FP8X4),
+                                    rhs_scale=tsg[TAB_ROW:P, c * CHUNK : (c + 1) * CHUNK], start=True, stop=True)
+            ht = sb.tile([P, CHUNK, PACK], F32, name=f"ht{c}")
+            nc.scalar.activation(ht[:], zh[:].rearrange("p t n -> p n t"), ACT.Tanh)
+            hint = sb.tile([P, CHUNK * PACK], BF16, name=f"hint{c}", align_bytes=64)
+            nc.vector.tensor_tensor(hint[:].rearrange("p (n t) -> p n t", t=PACK), ht[:], gh[:].unsqueeze(1).to_broadcast([P, CHUNK, PACK]), ALU.mult)
+            hc, hs = quantise(f"h{c}", hint[:], CHUNK)
+            nc.tensor.matmul_mx(out=c_ps[h][:, cols], lhsT=gc[:].bitcast(FP8X4), lhsT_scale=gsc[:], rhs=hc[:].bitcast(FP8X4), rhs_scale=hs[:], start=True, stop=True)
+
+        old_sb = sb.tile([P, T], F32, name="old_sb", tag="keys", align_bytes=64)
+        nc.sync.dma_start(old_sb[:], old)
+
+        sa = sb.tile([P, G], F32, name="sa")
+        nc.vector.tensor_reduce(sa[:], grouped(a_ps[:]), AX.X, ALU.add)
+        nms = sb.tile([P, G], F32, name="nms")
+        nmax = sb.tile([P, 1], F32, name="nmax")
+        nc.vector.tensor_scalar(nms[:], sa[:], nsh8[:], None, ALU.mult, ALU.min, accum_out=nmax[:])
+        s = sb.tile([P, G], F32, name="s")
+        nc.vector.tensor_reduce(s[:], grouped(p_sb[:]), AX.X, ALU.add)
+        pg = sb.tile([P, G], F32, name="pg")
+        z = sb.tile([P, 1], F32, name="z")
+        nc.scalar.activation(pg[:], nms[:], ACT.Exp, bias=nmax[:], scale=-1.0, accum_out=z[:])
+        rs = sb.tile([P, G], F32, name="rs")
+        nc.vector.reciprocal(rs[:], s[:])
+        rz = sb.tile([P, 1], F32, name="rz")
+        nc.vector.reciprocal(rz[:], z[:])
+        wneg = sb.tile([P, G], F32, name="wneg")
+        nc.vector.tensor_scalar(wneg[:], pg[:], rz[:], -512.0, ALU.mult, ALU.mult)
+        cg = sb.tile([P, G], F32, name="cg")
+        nc.vector.tensor_scalar(cg[:], pg[:], rz[:], nsh8[:], ALU.mult, ALU.mult)
+        npn = sb.tile([P, I], F32, name="npn", tag="tab")
+        nc.vector.scalar_tensor_tensor(grouped(npn[:]), grouped(p_sb[:]), -1.0, rep(rs[:], G), ALU.mult, ALU.mult)
+        pw = sb.tile([P, I], F32, name="pw")
+        nc.vector.tensor_tensor(grouped(pw[:]), grouped(npn[:]), rep(wneg[:], G), ALU.mult)
+
+        t1 = sb.tile([P, I], F32, name="t1")
+        d1 = sb.tile([P, I], F32, name="d1")
+        u = sb.tile([P, G], F32, name="u")
+        usum = [sb.tile([P, 1], F32, name=f"usum{h}") for h in range(2)]
+        for h in range(2):
+            sl = slice(h * HALF, (h + 1) * HALF)
+            gl = slice(h * G // 2, (h + 1) * G // 2)
+            nc.vector.scalar_tensor_tensor(t1[:, sl], c_ps[h][:], 1.0, pw[:, sl], ALU.mult, ALU.mult, accum_out=usum[h][:])
+            nc.vector.tensor_reduce(u[:, gl], grouped(t1[:, sl]), AX.X, ALU.add)
+            nc.vector.scalar_tensor_tensor(grouped(d1[:, sl]), grouped(npn[:, sl]), sh8[:], rep(u[:, gl], G // 2), ALU.add, ALU.mult)
+
+        utot = sb.tile([P, 1], F32, name="utot")
+        nc.vector.tensor_tensor(utot[:], usum[0][:], usum[1][:], ALU.add)
+        f = sb.tile([P, I], F32, name="f")
+        nc.vector.scalar_tensor_tensor(grouped(f[:]), rep(cg[:], G), utot[:], grouped(t1[:]), ALU.mult, ALU.add)
+        nc.vector.tensor_tensor(window[:].indirect(offsets[:]), f[:], d1[:], ALU.add)
+
+        for n in range(T // OUT_PIECE):
+            cols = slice(n * OUT_PIECE, (n + 1) * OUT_PIECE)
+            res = sb.tile([P, OUT_PIECE], F32, name=f"res{n}")
+            nc.vector.tensor_tensor(res[:], window[:, cols], old_sb[:, cols], ALU.add)
+            nc.sync.dma_start(out[:, cols], res[:])

@@ -1,6 +1,7 @@
 from contextlib import ExitStack
 
 import concourse.mybir as mybir
+from concourse.masks import make_identity
 
 D, K, R, T, I, Q, G = 512, 512, 512, 2048, 512, 128, 64
 FLOPS = 2 * D * Q * I + 2 * K * R * I + 2 * R * Q * I
@@ -24,13 +25,25 @@ HALF = I // 2
 TAB_ROW = 4
 OUT_PIECE = 512
 
+KEYS_AT = 0
+TAB_AT = 8192
+WC_AT = 16384
+W1_AT = 20480
+W0_AT = 24576
+TS_AT = 28672
+WINT_AT = 30720
+
 
 def tile_attend_blrgained_bygroup_kernel(tc, query, keys_words, keys_scales, sharp, tab_words, tab_scales, w1, gain, gout, hsc, old, offs, out):
     nc = tc.nc
 
     with ExitStack() as ctx:
         sb = ctx.enter_context(tc.tile_pool(name="sb", bufs=1))
+        lay = ctx.enter_context(tc.tile_pool(name="lay", bufs=1))
         ps = ctx.enter_context(tc.psum_pool(name="ps", bufs=1))
+
+        def placed(name, shape, dtype, at):
+            return lay.tile(shape, dtype, name=name, align_bytes=64, offset=at)
 
         def rep(ap, groups):
             return ap.unsqueeze(2).to_broadcast([P, groups, GS])
@@ -38,18 +51,22 @@ def tile_attend_blrgained_bygroup_kernel(tc, query, keys_words, keys_scales, sha
         def grouped(ap):
             return ap.rearrange("p (g e) -> p g e", e=GS)
 
-        def load_scales(queue, plane, scales, first):
+        def load_scales(plane, scales, first):
             for r in range(4):
-                queue.dma_start(plane[first + r : P : 32, :].bitcast(I32), scales[0, r:16:4, :].bitcast(I32))
+                nc.sync.dma_start(plane[first + r : P : 32, :].bitcast(I32), scales[0, r:16:4, :].bitcast(I32))
 
-        def quantise(name, inter, width):
-            codes = sb.tile([P, width], U32, name=name + "_codes", align_bytes=64)
-            scales = sb.tile([P, width], U8, name=name + "_scales", align_bytes=64)
-            nc.vector.quantize_mx(out=codes[:].bitcast(FP8X4), scales=scales[:], in_=inter)
-            return codes, scales
+        def quantise(name, inter, codes):
+            scales = sb.tile(list(codes.shape), U8, name=name, align_bytes=64)
+            nc.vector.quantize_mx(out=codes[:].bitcast(FP8X4), scales=scales[:], in_=inter[:])
+            return scales
+
+        def interleave(dst, src):
+            nc.scalar.copy(dst[:].rearrange("p (c i j) -> p c j i", i=4, j=PACK), src[:].rearrange("p j (c i) -> p c j i", i=4))
 
         offsets = sb.tile([P, I // 16], U16, name="offsets")
         nc.sync.dma_start(offsets[:], offs)
+        sharp_sb = sb.tile([P, 1], F32, name="sharp_sb")
+        nc.scalar.dma_start(sharp_sb[:], sharp)
 
         kscale = sb.tile([P, T], U8, name="kscale", align_bytes=64)
         tscale = sb.tile([P, T], U8, name="tscale", align_bytes=64)
@@ -57,30 +74,30 @@ def tile_attend_blrgained_bygroup_kernel(tc, query, keys_words, keys_scales, sha
         nc.vector.memset(tscale[:].bitcast(I32), 0)
         window = sb.tile([P, T], F32, name="window")
         nc.vector.memset(window[:], 0.0)
-        load_scales(nc.scalar, kscale, keys_scales, 0)
 
+        kwords = placed("kwords", [P, T], I32, KEYS_AT)
+        keys_flat = keys_words[0].rearrange("p n t -> p (n t)").bitcast(I32)
+        nc.sync.dma_start(kwords[:, : T // 2], keys_flat[:, : T // 2])
+        load_scales(kscale, keys_scales, 0)
+        nc.sync.dma_start(kwords[:, T // 2 :], keys_flat[:, T // 2 :])
         qraw = sb.tile([P, PACK, Q], F32, name="qraw", tag="raw")
         nc.sync.dma_start(qraw[:], query.rearrange("(p j) q -> p j q", j=PACK))
-        kwords = sb.tile([P, T], I32, name="kwords", tag="keys", align_bytes=64)
-        nc.sync.dma_start(kwords[:], keys_words[0].rearrange("p n t -> p (n t)").bitcast(I32))
-        wraw = []
-        for h in range(2):
-            wr = sb.tile([P, PACK, R // 2], F32, name=f"wraw{h}")
-            nc.sync.dma_start(wr[:], w1[:, h * R // 2 : (h + 1) * R // 2].rearrange("(p j) r -> p j r", j=PACK))
-            wraw.append(wr)
-        twords = sb.tile([P, T], I32, name="twords", tag="tab")
+        wraw = [placed("wraw0", [P, PACK, R // 2], F32, W0_AT), sb.tile([P, PACK, R // 2], F32, name="wraw1")]
+        w1_view = w1.rearrange("(p j) r -> p j r", j=PACK)
+        nc.sync.dma_start(wraw[0][:], w1_view[:, :, : R // 2])
+        load_scales(tscale, tab_scales, TAB_ROW)
+        nc.sync.dma_start(wraw[1][:], w1_view[:, :, R // 2 :])
+        twords = placed("twords", [P, T], I32, TAB_AT)
         nc.sync.dma_start(twords[:], tab_words[0].rearrange("p n t -> p (n t)").bitcast(I32))
-
-        sharp_sb = sb.tile([P, 1], F32, name="sharp_sb")
-        nc.gpsimd.dma_start(sharp_sb[:], sharp)
-        load_scales(nc.gpsimd, tscale, tab_scales, TAB_ROW)
         gain_sb = sb.tile([P, PACK], F32, name="gain_sb")
-        nc.gpsimd.dma_start(gain_sb[:], gain.rearrange("(p j) o -> p (j o)", j=PACK))
+        nc.sync.dma_start(gain_sb[:], gain.rearrange("(p j) o -> p (j o)", j=PACK))
         hsc_sb = sb.tile([P, PACK], F32, name="hsc_sb")
-        nc.gpsimd.dma_start(hsc_sb[:], hsc.rearrange("(p j) o -> p (j o)", j=PACK))
+        nc.sync.dma_start(hsc_sb[:], hsc.rearrange("(p j) o -> p (j o)", j=PACK))
         gh = sb.tile([P, PACK], F32, name="gh")
         nc.gpsimd.tensor_tensor(gh[:], gain_sb[:], hsc_sb[:], ALU.mult)
 
+        ident = sb.tile([P, P], F32, name="ident")
+        make_identity(nc, ident[:])
         sh8 = sb.tile([P, 1], F32, name="sh8")
         nc.scalar.activation(sh8[:], sharp_sb[:], ACT.Identity, scale=1.0 / GS)
         nsh8 = sb.tile([P, 1], F32, name="nsh8")
@@ -91,34 +108,68 @@ def tile_attend_blrgained_bygroup_kernel(tc, query, keys_words, keys_scales, sha
         kwg = sb.tile([P, I], U32, name="kwg", align_bytes=64)
         nc.vector.tensor_copy(kwg[:], kwords[:].bitcast(U32).indirect(offsets[:]))
         qint = sb.tile([P, Q * PACK], BF16, name="qint", align_bytes=64)
-        nc.scalar.copy(qint[:].rearrange("p (c i j) -> p c j i", i=4, j=PACK), qraw[:].rearrange("p j (c i) -> p c j i", i=4))
-        qc, qs = quantise("q", qint[:], Q)
+        interleave(qint, qraw)
+        qc = placed("qc", [P, Q], U32, KEYS_AT)
+        qs = quantise("qs", qint, qc)
         a_ps = ps.tile([P, I], F32, name="a_ps")
         nc.tensor.matmul_mx(out=a_ps[:], lhsT=qc[:].bitcast(FP8X4), lhsT_scale=qs[:], rhs=kwg[:].bitcast(FP8X4), rhs_scale=ksg[:], start=True, stop=True)
-        p_sb = sb.tile([P, I], F32, name="p_sb")
-        nc.scalar.activation(p_sb[:], a_ps[:], ACT.Exp)
 
         graw = sb.tile([P, PACK, Q], F32, name="graw", tag="raw")
         nc.sync.dma_start(graw[:], gout.rearrange("(p j) q -> p j q", j=PACK))
 
-        tsg = sb.tile([P, I], U8, name="tsg", tag="keys", align_bytes=64)
+        tsg = placed("tsg", [P, I], U8, KEYS_AT + 4096)
         nc.vector.tensor_copy(tsg[:], tscale[:].indirect(offsets[:]))
+
         wint = sb.tile([P, R * PACK], BF16, name="wint", align_bytes=64)
-        wv_out = wint[:].rearrange("p (t m j) -> p m t j", t=PACK, j=PACK)
+        wv_out = wint[:].rearrange("p (t m j) -> p m j t", t=PACK, j=PACK)
+        nc.scalar.copy(wv_out[:, 0:64], wraw[0][:].rearrange("p j (m t) -> p m j t", t=PACK))
+
+        dealt = placed("dealt", [P, GS, 2 * G], F32, W0_AT)
+        a_dealt = a_ps[:].rearrange("p (g e) -> p e g", e=GS)
         for h in range(2):
-            nc.scalar.copy(wv_out[:, 64 * h : 64 * (h + 1)], wraw[h][:].rearrange("p j (m t) -> p m t j", t=PACK))
-        wc, ws = quantise("w", wint[:], R)
+            es = slice(h * GS // 2, (h + 1) * GS // 2)
+            nc.scalar.activation(dealt[:, es, :G], a_dealt[:, es], ACT.Exp)
+            nc.scalar.copy(dealt[:, es, G:], a_dealt[:, es])
+        p_sb = sb.tile([P, I], F32, name="p_sb")
+        nc.scalar.activation(p_sb[:], a_ps[:], ACT.Exp)
+        sums_t_ps = ps.tile([P, P], F32, name="sums_t_ps")
+        for e in range(GS):
+            nc.tensor.matmul(sums_t_ps[:], dealt[:, e, :], ident[:], start=(e == 0), stop=(e == GS - 1), is_transpose=True)
+        sums_t = sb.tile([P, P], F32, name="sums_t")
+        nc.scalar.copy(sums_t[:], sums_t_ps[:])
+        sums = ps.tile([P, P], F32, name="sums", tag="c_ps1")
+        nc.tensor.transpose(sums[:], sums_t[:], ident[:])
+
+        nc.vector.tensor_copy(wv_out[:, 64:128], wraw[1][:].rearrange("p j (m t) -> p m j t", t=PACK))
+        wc = sb.tile([P, R], U32, name="wc", align_bytes=64)
+        ws = quantise("ws", wint, wc)
+        tab_view = twords[:].bitcast(U32)
         twg = []
         for h in range(2):
-            tw = sb.tile([P, HALF], U32, name=f"twg{h}", align_bytes=64)
-            nc.vector.tensor_copy(tw[:], twords[:].bitcast(U32).indirect(offsets[:, 16 * h : 16 * (h + 1)]))
-            twg.append(tw)
+            twg.append(sb.tile([P, HALF], U32, name=f"twg{h}", align_bytes=64))
+            nc.vector.tensor_copy(twg[h][:], tab_view.indirect(offsets[:, 16 * h : 16 * (h + 1)]))
+
+        rs = placed("rs", [P, G], F32, TAB_AT + 256)
+        nc.vector.reciprocal(rs[:], sums[:, :G])
+        npn = sb.tile([P, I], F32, name="npn")
+        nc.vector.scalar_tensor_tensor(grouped(npn[:]), grouped(p_sb[:]), -1.0, rep(rs[:], G), ALU.mult, ALU.mult)
+        nms = placed("nms", [P, G], F32, TAB_AT)
+        nmax = sb.tile([P, 1], F32, name="nmax")
+        nc.vector.tensor_scalar(nms[:], sums[:, G:], nsh8[:], None, ALU.mult, ALU.min, accum_out=nmax[:])
+        pg = sb.tile([P, G], F32, name="pg")
+        z = sb.tile([P, 1], F32, name="z")
+        nc.scalar.activation(pg[:], nms[:], ACT.Exp, bias=nmax[:], scale=-1.0, accum_out=z[:])
+        rz = sb.tile([P, 1], F32, name="rz")
+        nc.vector.reciprocal(rz[:], z[:])
+        pw = sb.tile([P, I], F32, name="pw")
+        nc.vector.scalar_tensor_tensor(grouped(pw[:]), grouped(npn[:]), rz[:], rep(pg[:], G), ALU.mult, ALU.mult)
 
         gint = sb.tile([P, Q * PACK], BF16, name="gint", align_bytes=64)
-        nc.scalar.copy(gint[:].rearrange("p (c i j) -> p c j i", i=4, j=PACK), graw[:].rearrange("p j (c i) -> p c j i", i=4))
-        gc, gsc = quantise("g", gint[:], Q)
+        interleave(gint, graw)
+        gc = placed("gc", [P, Q], U32, TAB_AT + 2048)
+        gsc = quantise("gsc", gint, gc)
 
-        c_ps = [ps.tile([P, HALF], F32, name=f"c_ps{h}") for h in range(2)]
+        c_ps = [ps.tile([P, HALF], F32, name=f"c_ps{h}", tag=f"c_ps{h}") for h in range(2)]
         for c in range(I // CHUNK):
             h, e = divmod(c, 2)
             cols = slice(e * CHUNK, (e + 1) * CHUNK)
@@ -131,35 +182,15 @@ def tile_attend_blrgained_bygroup_kernel(tc, query, keys_words, keys_scales, sha
             nc.scalar.activation(ht[:], zh[:].rearrange("p t n -> p n t"), ACT.Tanh)
             hint = sb.tile([P, CHUNK * PACK], BF16, name=f"hint{c}", align_bytes=64)
             nc.vector.tensor_tensor(hint[:].rearrange("p (n t) -> p n t", t=PACK), ht[:], gh[:].unsqueeze(1).to_broadcast([P, CHUNK, PACK]), ALU.mult)
-            hc, hs = quantise(f"h{c}", hint[:], CHUNK)
+            hc = sb.tile([P, CHUNK], U32, name=f"hc{c}", align_bytes=64)
+            hs = quantise(f"hs{c}", hint, hc)
             nc.tensor.matmul_mx(out=c_ps[h][:, cols], lhsT=gc[:].bitcast(FP8X4), lhsT_scale=gsc[:], rhs=hc[:].bitcast(FP8X4), rhs_scale=hs[:], start=True, stop=True)
 
-        old_sb = sb.tile([P, T], F32, name="old_sb", tag="keys", align_bytes=64)
+        old_sb = placed("old_sb", [P, T], F32, KEYS_AT)
         nc.sync.dma_start(old_sb[:], old)
 
-        sa = sb.tile([P, G], F32, name="sa")
-        nc.vector.tensor_reduce(sa[:], grouped(a_ps[:]), AX.X, ALU.add)
-        nms = sb.tile([P, G], F32, name="nms")
-        nmax = sb.tile([P, 1], F32, name="nmax")
-        nc.vector.tensor_scalar(nms[:], sa[:], nsh8[:], None, ALU.mult, ALU.min, accum_out=nmax[:])
-        s = sb.tile([P, G], F32, name="s")
-        nc.vector.tensor_reduce(s[:], grouped(p_sb[:]), AX.X, ALU.add)
-        pg = sb.tile([P, G], F32, name="pg")
-        z = sb.tile([P, 1], F32, name="z")
-        nc.scalar.activation(pg[:], nms[:], ACT.Exp, bias=nmax[:], scale=-1.0, accum_out=z[:])
-        rs = sb.tile([P, G], F32, name="rs")
-        nc.vector.reciprocal(rs[:], s[:])
-        rz = sb.tile([P, 1], F32, name="rz")
-        nc.vector.reciprocal(rz[:], z[:])
-        wneg = sb.tile([P, G], F32, name="wneg")
-        nc.vector.tensor_scalar(wneg[:], pg[:], rz[:], -512.0, ALU.mult, ALU.mult)
-        cg = sb.tile([P, G], F32, name="cg")
-        nc.vector.tensor_scalar(cg[:], pg[:], rz[:], nsh8[:], ALU.mult, ALU.mult)
-        npn = sb.tile([P, I], F32, name="npn", tag="tab")
-        nc.vector.scalar_tensor_tensor(grouped(npn[:]), grouped(p_sb[:]), -1.0, rep(rs[:], G), ALU.mult, ALU.mult)
-        pw = sb.tile([P, I], F32, name="pw")
-        nc.vector.tensor_tensor(grouped(pw[:]), grouped(npn[:]), rep(wneg[:], G), ALU.mult)
-
+        cu = sb.tile([P, 1], F32, name="cu")
+        nc.scalar.activation(cu[:], rz[:], ACT.Copy, scale=nsh8[:])
         t1 = sb.tile([P, I], F32, name="t1")
         d1 = sb.tile([P, I], F32, name="d1")
         u = sb.tile([P, G], F32, name="u")
@@ -167,14 +198,14 @@ def tile_attend_blrgained_bygroup_kernel(tc, query, keys_words, keys_scales, sha
         for h in range(2):
             sl = slice(h * HALF, (h + 1) * HALF)
             gl = slice(h * G // 2, (h + 1) * G // 2)
-            nc.vector.scalar_tensor_tensor(t1[:, sl], c_ps[h][:], 1.0, pw[:, sl], ALU.mult, ALU.mult, accum_out=usum[h][:])
+            nc.vector.scalar_tensor_tensor(t1[:, sl], c_ps[h][:], -512.0, pw[:, sl], ALU.mult, ALU.mult, accum_out=usum[h][:])
             nc.vector.tensor_reduce(u[:, gl], grouped(t1[:, sl]), AX.X, ALU.add)
             nc.vector.scalar_tensor_tensor(grouped(d1[:, sl]), grouped(npn[:, sl]), sh8[:], rep(u[:, gl], G // 2), ALU.add, ALU.mult)
 
         utot = sb.tile([P, 1], F32, name="utot")
-        nc.vector.tensor_tensor(utot[:], usum[0][:], usum[1][:], ALU.add)
+        nc.vector.tensor_scalar(utot[:], usum[0][:], usum[1][:], cu[:], ALU.add, ALU.mult)
         f = sb.tile([P, I], F32, name="f")
-        nc.vector.scalar_tensor_tensor(grouped(f[:]), rep(cg[:], G), utot[:], grouped(t1[:]), ALU.mult, ALU.add)
+        nc.vector.scalar_tensor_tensor(grouped(f[:]), rep(pg[:], G), utot[:], grouped(t1[:]), ALU.mult, ALU.add)
         nc.vector.tensor_tensor(window[:].indirect(offsets[:]), f[:], d1[:], ALU.add)
 
         for n in range(T // OUT_PIECE):

from contextlib import ExitStack

import concourse.mybir as mybir
from concourse.masks import make_identity

D, K, R, T, I, Q, G = 512, 512, 512, 2048, 512, 128, 64
FLOPS = 2 * D * Q * I + 2 * K * R * I + 2 * R * Q * I

F32 = mybir.dt.float32
BF16 = mybir.dt.bfloat16
I32 = mybir.dt.int32
U32 = mybir.dt.uint32
U16 = mybir.dt.uint16
U8 = mybir.dt.uint8
FP8X4 = mybir.dt.float8_e4m3fn_x4
ALU = mybir.AluOpType
ACT = mybir.ActivationFunctionType
AX = mybir.AxisListType

P = 128
PACK = 4
GS = I // G
CHUNK = 128
HALF = I // 2
TAB_ROW = 4
OUT_PIECE = 512

KEYS_AT = 0
TAB_AT = 8192
WC_AT = 16384
W1_AT = 20480
W0_AT = 24576
TS_AT = 28672
WINT_AT = 30720


def tile_attend_blrgained_bygroup_kernel(tc, query, keys_words, keys_scales, sharp, tab_words, tab_scales, w1, gain, gout, hsc, old, offs, out):
    nc = tc.nc

    with ExitStack() as ctx:
        sb = ctx.enter_context(tc.tile_pool(name="sb", bufs=1))
        lay = ctx.enter_context(tc.tile_pool(name="lay", bufs=1))
        ps = ctx.enter_context(tc.psum_pool(name="ps", bufs=1))

        def placed(name, shape, dtype, at):
            return lay.tile(shape, dtype, name=name, align_bytes=64, offset=at)

        def rep(ap, groups):
            return ap.unsqueeze(2).to_broadcast([P, groups, GS])

        def grouped(ap):
            return ap.rearrange("p (g e) -> p g e", e=GS)

        def load_scales(plane, scales, first):
            for r in range(4):
                nc.sync.dma_start(plane[first + r : P : 32, :].bitcast(I32), scales[0, r:16:4, :].bitcast(I32))

        def quantise(name, inter, codes):
            scales = sb.tile(list(codes.shape), U8, name=name, align_bytes=64)
            nc.vector.quantize_mx(out=codes[:].bitcast(FP8X4), scales=scales[:], in_=inter[:])
            return scales

        def interleave(dst, src):
            nc.scalar.copy(dst[:].rearrange("p (c i j) -> p c j i", i=4, j=PACK), src[:].rearrange("p j (c i) -> p c j i", i=4))

        offsets = sb.tile([P, I // 16], U16, name="offsets")
        nc.sync.dma_start(offsets[:], offs)
        sharp_sb = sb.tile([P, 1], F32, name="sharp_sb")
        nc.scalar.dma_start(sharp_sb[:], sharp)

        kscale = sb.tile([P, T], U8, name="kscale", align_bytes=64)
        tscale = sb.tile([P, T], U8, name="tscale", align_bytes=64)
        nc.vector.memset(kscale[:].bitcast(I32), 0)
        nc.vector.memset(tscale[:].bitcast(I32), 0)
        window = sb.tile([P, T], F32, name="window")
        nc.vector.memset(window[:], 0.0)

        kwords = placed("kwords", [P, T], I32, KEYS_AT)
        keys_flat = keys_words[0].rearrange("p n t -> p (n t)").bitcast(I32)
        nc.sync.dma_start(kwords[:, : T // 2], keys_flat[:, : T // 2])
        load_scales(kscale, keys_scales, 0)
        nc.sync.dma_start(kwords[:, T // 2 :], keys_flat[:, T // 2 :])
        qraw = sb.tile([P, PACK, Q], F32, name="qraw", tag="raw")
        nc.sync.dma_start(qraw[:], query.rearrange("(p j) q -> p j q", j=PACK))
        wraw = [placed("wraw0", [P, PACK, R // 2], F32, W0_AT), sb.tile([P, PACK, R // 2], F32, name="wraw1")]
        w1_view = w1.rearrange("(p j) r -> p j r", j=PACK)
        nc.sync.dma_start(wraw[0][:], w1_view[:, :, : R // 2])
        load_scales(tscale, tab_scales, TAB_ROW)
        nc.sync.dma_start(wraw[1][:], w1_view[:, :, R // 2 :])
        twords = placed("twords", [P, T], I32, TAB_AT)
        nc.sync.dma_start(twords[:], tab_words[0].rearrange("p n t -> p (n t)").bitcast(I32))
        gain_sb = sb.tile([P, PACK], F32, name="gain_sb")
        nc.sync.dma_start(gain_sb[:], gain.rearrange("(p j) o -> p (j o)", j=PACK))
        hsc_sb = sb.tile([P, PACK], F32, name="hsc_sb")
        nc.sync.dma_start(hsc_sb[:], hsc.rearrange("(p j) o -> p (j o)", j=PACK))
        gh = sb.tile([P, PACK], F32, name="gh")
        nc.gpsimd.tensor_tensor(gh[:], gain_sb[:], hsc_sb[:], ALU.mult)

        ident = sb.tile([P, P], F32, name="ident")
        make_identity(nc, ident[:])
        sh8 = sb.tile([P, 1], F32, name="sh8")
        nc.scalar.activation(sh8[:], sharp_sb[:], ACT.Identity, scale=1.0 / GS)
        nsh8 = sb.tile([P, 1], F32, name="nsh8")
        nc.scalar.activation(nsh8[:], sharp_sb[:], ACT.Identity, scale=-1.0 / GS)

        ksg = sb.tile([P, I], U8, name="ksg", align_bytes=64)
        nc.vector.tensor_copy(ksg[:], kscale[:].indirect(offsets[:]))
        kwg = sb.tile([P, I], U32, name="kwg", align_bytes=64)
        nc.vector.tensor_copy(kwg[:], kwords[:].bitcast(U32).indirect(offsets[:]))
        qint = sb.tile([P, Q * PACK], BF16, name="qint", align_bytes=64)
        interleave(qint, qraw)
        qc = placed("qc", [P, Q], U32, KEYS_AT)
        qs = quantise("qs", qint, qc)
        a_ps = ps.tile([P, I], F32, name="a_ps")
        nc.tensor.matmul_mx(out=a_ps[:], lhsT=qc[:].bitcast(FP8X4), lhsT_scale=qs[:], rhs=kwg[:].bitcast(FP8X4), rhs_scale=ksg[:], start=True, stop=True)

        graw = sb.tile([P, PACK, Q], F32, name="graw", tag="raw")
        nc.sync.dma_start(graw[:], gout.rearrange("(p j) q -> p j q", j=PACK))

        tsg = placed("tsg", [P, I], U8, KEYS_AT + 4096)
        nc.vector.tensor_copy(tsg[:], tscale[:].indirect(offsets[:]))

        wint = sb.tile([P, R * PACK], BF16, name="wint", align_bytes=64)
        wv_out = wint[:].rearrange("p (t m j) -> p m j t", t=PACK, j=PACK)
        nc.scalar.copy(wv_out[:, 0:64], wraw[0][:].rearrange("p j (m t) -> p m j t", t=PACK))

        dealt = placed("dealt", [P, GS, 2 * G], F32, W0_AT)
        a_dealt = a_ps[:].rearrange("p (g e) -> p e g", e=GS)
        for h in range(2):
            es = slice(h * GS // 2, (h + 1) * GS // 2)
            nc.scalar.activation(dealt[:, es, :G], a_dealt[:, es], ACT.Exp)
            nc.scalar.copy(dealt[:, es, G:], a_dealt[:, es])
        p_sb = sb.tile([P, I], F32, name="p_sb")
        nc.scalar.activation(p_sb[:], a_ps[:], ACT.Exp)
        sums_t_ps = ps.tile([P, P], F32, name="sums_t_ps")
        for e in range(GS):
            nc.tensor.matmul(sums_t_ps[:], dealt[:, e, :], ident[:], start=(e == 0), stop=(e == GS - 1), is_transpose=True)
        sums_t = sb.tile([P, P], F32, name="sums_t")
        nc.scalar.copy(sums_t[:], sums_t_ps[:])
        sums = ps.tile([P, P], F32, name="sums", tag="c_ps1")
        nc.tensor.transpose(sums[:], sums_t[:], ident[:])

        nc.vector.tensor_copy(wv_out[:, 64:128], wraw[1][:].rearrange("p j (m t) -> p m j t", t=PACK))
        wc = sb.tile([P, R], U32, name="wc", align_bytes=64)
        ws = quantise("ws", wint, wc)
        tab_view = twords[:].bitcast(U32)
        twg = []
        for h in range(2):
            twg.append(sb.tile([P, HALF], U32, name=f"twg{h}", align_bytes=64))
            nc.vector.tensor_copy(twg[h][:], tab_view.indirect(offsets[:, 16 * h : 16 * (h + 1)]))

        rs = placed("rs", [P, G], F32, TAB_AT + 256)
        nc.vector.reciprocal(rs[:], sums[:, :G])
        npn = sb.tile([P, I], F32, name="npn")
        nc.vector.scalar_tensor_tensor(grouped(npn[:]), grouped(p_sb[:]), -1.0, rep(rs[:], G), ALU.mult, ALU.mult)
        nms = placed("nms", [P, G], F32, TAB_AT)
        nmax = sb.tile([P, 1], F32, name="nmax")
        nc.vector.tensor_scalar(nms[:], sums[:, G:], nsh8[:], None, ALU.mult, ALU.min, accum_out=nmax[:])
        pg = sb.tile([P, G], F32, name="pg")
        z = sb.tile([P, 1], F32, name="z")
        nc.scalar.activation(pg[:], nms[:], ACT.Exp, bias=nmax[:], scale=-1.0, accum_out=z[:])
        rz = sb.tile([P, 1], F32, name="rz")
        nc.vector.reciprocal(rz[:], z[:])
        pw = sb.tile([P, I], F32, name="pw")
        nc.vector.scalar_tensor_tensor(grouped(pw[:]), grouped(npn[:]), rz[:], rep(pg[:], G), ALU.mult, ALU.mult)

        gint = sb.tile([P, Q * PACK], BF16, name="gint", align_bytes=64)
        interleave(gint, graw)
        gc = placed("gc", [P, Q], U32, TAB_AT + 2048)
        gsc = quantise("gsc", gint, gc)

        c_ps = [ps.tile([P, HALF], F32, name=f"c_ps{h}", tag=f"c_ps{h}") for h in range(2)]
        for c in range(I // CHUNK):
            h, e = divmod(c, 2)
            cols = slice(e * CHUNK, (e + 1) * CHUNK)
            zh = ps.tile([P, PACK, CHUNK], F32, name=f"zh{c}")
            for t in range(PACK):
                m = slice(t * P, (t + 1) * P)
                nc.tensor.matmul_mx(out=zh[:, t, :], lhsT=wc[:, m].bitcast(FP8X4), lhsT_scale=ws[:, m], rhs=twg[h][:, cols].bitcast(FP8X4),
                                    rhs_scale=tsg[TAB_ROW:P, c * CHUNK : (c + 1) * CHUNK], start=True, stop=True)
            ht = sb.tile([P, CHUNK, PACK], F32, name=f"ht{c}")
            nc.scalar.activation(ht[:], zh[:].rearrange("p t n -> p n t"), ACT.Tanh)
            hint = sb.tile([P, CHUNK * PACK], BF16, name=f"hint{c}", align_bytes=64)
            nc.vector.tensor_tensor(hint[:].rearrange("p (n t) -> p n t", t=PACK), ht[:], gh[:].unsqueeze(1).to_broadcast([P, CHUNK, PACK]), ALU.mult)
            hc = sb.tile([P, CHUNK], U32, name=f"hc{c}", align_bytes=64)
            hs = quantise(f"hs{c}", hint, hc)
            nc.tensor.matmul_mx(out=c_ps[h][:, cols], lhsT=gc[:].bitcast(FP8X4), lhsT_scale=gsc[:], rhs=hc[:].bitcast(FP8X4), rhs_scale=hs[:], start=True, stop=True)

        old_sb = placed("old_sb", [P, T], F32, KEYS_AT)
        nc.sync.dma_start(old_sb[:], old)

        cu = sb.tile([P, 1], F32, name="cu")
        nc.scalar.activation(cu[:], rz[:], ACT.Copy, scale=nsh8[:])
        t1 = sb.tile([P, I], F32, name="t1")
        d1 = sb.tile([P, I], F32, name="d1")
        u = sb.tile([P, G], F32, name="u")
        usum = [sb.tile([P, 1], F32, name=f"usum{h}") for h in range(2)]
        for h in range(2):
            sl = slice(h * HALF, (h + 1) * HALF)
            gl = slice(h * G // 2, (h + 1) * G // 2)
            nc.vector.scalar_tensor_tensor(t1[:, sl], c_ps[h][:], -512.0, pw[:, sl], ALU.mult, ALU.mult, accum_out=usum[h][:])
            nc.vector.tensor_reduce(u[:, gl], grouped(t1[:, sl]), AX.X, ALU.add)
            nc.vector.scalar_tensor_tensor(grouped(d1[:, sl]), grouped(npn[:, sl]), sh8[:], rep(u[:, gl], G // 2), ALU.add, ALU.mult)

        utot = sb.tile([P, 1], F32, name="utot")
        nc.vector.tensor_scalar(utot[:], usum[0][:], usum[1][:], cu[:], ALU.add, ALU.mult)
        f = sb.tile([P, I], F32, name="f")
        nc.vector.scalar_tensor_tensor(grouped(f[:]), rep(pg[:], G), utot[:], grouped(t1[:]), ALU.mult, ALU.add)
        nc.vector.tensor_tensor(window[:].indirect(offsets[:]), f[:], d1[:], ALU.add)

        for n in range(T // OUT_PIECE):
            cols = slice(n * OUT_PIECE, (n + 1) * OUT_PIECE)
            res = sb.tile([P, OUT_PIECE], F32, name=f"res{n}")
            nc.vector.tensor_tensor(res[:], window[:, cols], old_sb[:, cols], ALU.add)
            nc.sync.dma_start(out[:, cols], res[:])
